import numpy as np
import ml_dtypes


def mxq(x, axis, fmt="e4m3"):
    dtype, down = {"e4m3": (ml_dtypes.float8_e4m3fn, 7), "e5m2": (ml_dtypes.float8_e5m2, 14)}[fmt]
    v = np.moveaxis(np.asarray(x, np.float32).astype(ml_dtypes.bfloat16).astype(np.float64), axis, -1)
    blocks = v.reshape(v.shape[:-1] + (-1, 32))
    amax = np.abs(blocks).max(-1, keepdims=True)
    byte = np.maximum(np.where(amax > 0, np.frexp(amax)[1] - 1 + 127, 0) - down, 1)
    scale = np.exp2(byte - 127.0)
    codes = (blocks / scale).astype(np.float32).astype(dtype).astype(np.float64)
    return np.moveaxis((codes * scale).reshape(v.shape), -1, axis)


WIDE = False


def mx_kscale(k):
    if not WIDE:
        return np.ones(k)
    levels = np.array([10, -10, 5, -5, 0])
    if k % 512:
        return np.exp2(np.random.permutation(np.resize(levels, k // 32))).repeat(32)
    a = np.empty((k // 512, 16))
    for p in range(k // 512):
        a[p, :8] = np.random.permutation(np.resize(levels, 8))
        for g in range(8):
            far = levels[np.abs(levels - a[p, g]) >= 10]
            a[p, g + 8] = far[np.random.randint(len(far))]
    return np.exp2(a.ravel()).repeat(32)


def f64(x):
    return np.asarray(x).astype(np.float64)


def striped(idx):
    return np.tile(np.asarray(idx).reshape(-1, 16).T, (8, 1)).astype(np.uint16)


def unstriped(offs):
    return offs[:16].T.reshape(-1).astype(np.int64)


E2M1 = np.array([0.0, 0.5, 1.0, 1.5, 2.0, 3.0, 4.0, 6.0, -0.0, -0.5, -1.0, -1.5, -2.0, -3.0, -4.0, -6.0])


def pack_weight(w, fmt):
    k, n = w.shape
    w = f64(np.asarray(w, np.float32).astype(ml_dtypes.bfloat16)).reshape(k // 32, 32, n)
    amax = np.abs(w).max(1)
    if fmt == "e4m3":
        byte = np.frexp(amax)[1] - 1 + 127 - 7
    else:
        mant, ex = np.frexp(amax / 6.0)
        byte = np.where(mant > 0.5, ex, ex - 1) + 127
    byte = np.clip(np.where(amax > 0, byte, 1), 1, 254)
    scaled = (w * np.exp2(127.0 - byte)[:, None, :]).reshape(k, n).astype(np.float32)
    by_word = np.ascontiguousarray(scaled.reshape(k // 512, 128, 4, n).transpose(0, 1, 3, 2))
    if fmt == "e4m3":
        words = by_word.astype(ml_dtypes.float8_e4m3fn).view(np.uint8)
    else:
        c = by_word.astype(ml_dtypes.float4_e2m1fn).view(np.uint8) & 0xF
        words = (c[..., 0::2] | (c[..., 1::2] << 4)).reshape(k // 512, 128, 2 * n)
    return np.ascontiguousarray(words), np.ascontiguousarray(byte.astype(np.uint8).reshape(k // 512, 16, n))


def unpack_weight(words, scales, fmt):
    g, _, n = scales.shape
    words = np.ascontiguousarray(words).reshape(g, 128, n, -1)
    if fmt == "e4m3":
        vals = words.view(ml_dtypes.float8_e4m3fn).astype(np.float64)
    else:
        nib = np.empty((g, 128, n, 4), np.uint8)
        nib[..., 0::2] = words & 0xF
        nib[..., 1::2] = words >> 4
        vals = E2M1[nib]
    vals = vals * np.repeat(np.exp2(scales.astype(np.float64) - 127.0), 8, axis=1)[..., None]
    return vals.transpose(0, 1, 3, 2).reshape(g * 512, n)


D, T, I, Q, E, K = 512, 2048, 512, 128, 512, 512


def setup_inputs():
    n = np.random.standard_normal
    idx = np.random.permutation(T)[:I]
    fd = mx_kscale(D)
    fk = mx_kscale(K)
    fi = mx_kscale(I)
    ti = np.ones(T)
    ti[idx] = fi
    keysp = pack_weight(n((D, T)) / fd[:, None], "e4m3")
    return {
        "query": (n((D, Q)) * 0.4 / np.sqrt(D) * fd[:, None]).astype(np.float32),
        "query2": (n((K, Q)) * 0.4 / np.sqrt(K) * fk[:, None]).astype(np.float32),
        "keys_words": keysp[0],
        "keys_scales": keysp[1],
        "keys2": (n((K, T)) / fk[:, None]).astype(np.float32),
        "size": (np.random.uniform(0.5, 2.0, (1, I)) * fi).astype(np.float32),
        "vals": (n((E, T)) / ti).astype(np.float32),
        "offs": striped(idx),
    }


def reference(query, query2, keys_words, keys_scales, keys2, size, vals, offs):
    idx = unstriped(offs)
    keysu = unpack_weight(keys_words, keys_scales, "e4m3")
    queryq = mxq(f64(query), 0, "e4m3")
    keysidxg = keysu[:, idx]
    a = queryq.T @ keysidxg
    query2q = mxq(f64(query2), 0, "e4m3")
    keys2idxq = mxq(f64(keys2)[:, idx], 0, "e4m3")
    b = query2q.T @ keys2idxq
    s = np.maximum(a, b) + np.minimum(a, b) * 0.5
    p = np.exp(s - np.max(s, axis=1, keepdims=True))
    w = p * f64(size) / np.sum(p, axis=1, keepdims=True)
    wt = w.T
    vt = f64(vals)[:, idx].T
    wtq = mxq(wt, 0, "e4m3")
    vtq = mxq(vt, 0, "e4m3")
    o = wtq.T @ vtq
    return o

@@ -1,0 +1,146 @@
+from contextlib import ExitStack
+
+import concourse.mybir as mybir
+from concourse.masks import make_identity
+
+D, T, I, Q, E, K = 512, 2048, 512, 128, 512, 512
+FLOPS = 2 * Q * I * (D + K + E)
+
+F32 = mybir.dt.float32
+BF16 = mybir.dt.bfloat16
+I32 = mybir.dt.int32
+U32 = mybir.dt.uint32
+U16 = mybir.dt.uint16
+U8 = mybir.dt.uint8
+FP8X4 = mybir.dt.float8_e4m3fn_x4
+ALU = mybir.AluOpType
+ACT = mybir.ActivationFunctionType
+AX = mybir.AxisListType
+
+P = 128
+PACK = 4
+
+
+def tile_attend_bestofviews_kernel(tc, query, query2, keys_words, keys_scales, keys2, size, vals, offs, out):
+    nc = tc.nc
+    with ExitStack() as ctx:
+        held = ctx.enter_context(tc.tile_pool(name="held", bufs=1))
+        psum = ctx.enter_context(tc.psum_pool(name="psum", bufs=1))
+        psum2 = ctx.enter_context(tc.psum_pool(name="psum2", bufs=2))
+
+        offsets = held.tile([P, I // 16], U16, name="offsets")
+        key2_pool = [held.tile([P, T], F32, name="key2_pool%d" % t) for t in range(PACK)]
+        val_pool = [held.tile([P, T], F32, name="val_pool%d" % j) for j in range(E // P)]
+        word_pool = held.tile([P, T], I32, name="word_pool")
+        scale_pool = held.tile([P, T], U8, name="scale_pool")
+        q_raw = [held.tile([P, PACK, Q], F32, name="q_raw%d" % v) for v in range(2)]
+        size_col = held.tile([P, PACK], F32, name="size_col")
+
+        keys2_planes = keys2.rearrange("(p t) n -> t p n", t=PACK)
+        nc.sync.dma_start(key2_pool[0][:], keys2_planes[0])
+        nc.sync.dma_start(offsets[:], offs)
+        for t in range(1, 3):
+            nc.sync.dma_start(key2_pool[t][:], keys2_planes[t])
+        nc.vector.memset(scale_pool[:].bitcast(I32), 0)
+        for g in range(4):
+            nc.sync.dma_start(
+                scale_pool[32 * g : 32 * g + 4, :].bitcast(I32),
+                keys_scales[0, 4 * g : 4 * g + 4, :].bitcast(I32),
+            )
+        nc.sync.dma_start(size_col[:], size.rearrange("o (p t) -> (o p) t", t=PACK))
+        nc.sync.dma_start(key2_pool[3][:], keys2_planes[3])
+        nc.sync.dma_start(q_raw[1][:], query2.rearrange("(p t) q -> p t q", t=PACK))
+        nc.sync.dma_start(q_raw[0][:], query.rearrange("(p t) q -> p t q", t=PACK))
+        nc.sync.dma_start(word_pool[:], keys_words[0].rearrange("p n t -> p (n t)").bitcast(I32))
+        for j in range(E // P):
+            nc.sync.dma_start(val_pool[j][:], vals[j * P : (j + 1) * P, :])
+
+
+        warm = held.tile([P, 2], F32, name="warm")
+        nc.vector.memset(warm[:, 0:1], 0.0)
+        nc.scalar.activation(warm[:, 1:2], warm[:, 0:1], ACT.Exp)
+
+        ident = held.tile([P, P], F32, name="ident")
+        make_identity(nc, ident[:])
+
+        size_rows = psum.tile([P, PACK, P], F32, name="size_rows")
+        for t in range(PACK):
+            nc.tensor.transpose(size_rows[:, t, :], size_col[:, t : t + 1].to_broadcast([P, P]), ident[:])
+
+        key_scales = held.tile([P, I], U8, name="key_scales", align_bytes=64)
+
+        key2_bf = held.tile([P, I, PACK], BF16, name="key2_bf", align_bytes=64)
+        for t in range(PACK):
+            nc.vector.tensor_copy(key2_bf[:, :, t], key2_pool[t][:].indirect(offsets[:]))
+            if t == 2:
+                nc.vector.tensor_copy(key_scales[:], scale_pool[:].indirect(offsets[:]))
+        key2_codes = held.tile([P, I], U32, name="key2_codes", align_bytes=64)
+        key2_scales = held.tile([P, I], U8, name="key2_scales", align_bytes=64)
+        nc.vector.quantize_mx(key2_codes[:].bitcast(FP8X4), key2_scales[:], key2_bf[:].rearrange("p i t -> p (i t)"))
+
+        q_bf = held.tile([P, 2, Q, PACK], BF16, name="q_bf", align_bytes=64)
+        for v in (1, 0):
+            nc.scalar.copy(q_bf[:, v], q_raw[v][:].rearrange("p t q -> p q t"))
+        q_codes = held.tile([P, 2 * Q], U32, name="q_codes", align_bytes=64)
+        q_scales = held.tile([P, 2 * Q], U8, name="q_scales", align_bytes=64)
+        nc.vector.quantize_mx(q_codes[:].bitcast(FP8X4), q_scales[:], q_bf[:].rearrange("p v q t -> p (v q t)"))
+
+        b_ps = psum.tile([P, I], F32, name="b_ps")
+        nc.tensor.matmul_mx(b_ps[:], q_codes[:, Q:].bitcast(FP8X4), q_scales[:, Q:],
+                            key2_codes[:].bitcast(FP8X4), key2_scales[:], start=True, stop=True)
+        b_sb = held.tile([P, I], F32, name="b_sb")
+        nc.scalar.copy(b_sb[:], b_ps[:])
+
+        key_codes = held.tile([P, I], U32, name="key_codes", align_bytes=64)
+        nc.vector.tensor_copy(key_codes[:], word_pool[:].bitcast(U32).indirect(offsets[:]))
+        a_ps = psum.tile([P, I], F32, name="a_ps")
+        nc.tensor.matmul_mx(a_ps[:], q_codes[:, :Q].bitcast(FP8X4), q_scales[:, :Q],
+                            key_codes[:].bitcast(FP8X4), key_scales[:], start=True, stop=True)
+
+        hi = held.tile([P, I], F32, name="hi")
+        lo = held.tile([P, I], F32, name="lo")
+        s = held.tile([P, I], F32, name="s")
+        nc.vector.tensor_tensor(hi[:], a_ps[:], b_sb[:], ALU.max)
+        nc.vector.tensor_tensor(lo[:], a_ps[:], b_sb[:], ALU.min)
+        nc.vector.scalar_tensor_tensor(s[:], lo[:], 0.5, hi[:], ALU.mult, ALU.add)
+        neg_max = held.tile([P, 1], F32, name="neg_max")
+        nc.vector.tensor_reduce(neg_max[:], s[:], AX.X, ALU.max, negate=True)
+        p_un = held.tile([P, I], F32, name="p_un")
+        row_sum = held.tile([P, 1], F32, name="row_sum")
+        nc.scalar.activation(p_un[:], s[:], ACT.Exp, bias=neg_max[:], scale=1.0, accum_out=row_sum[:])
+        inv_sum = held.tile([P, 1], F32, name="inv_sum")
+        nc.vector.reciprocal(inv_sum[:], row_sum[:])
+        w_bf = held.tile([P, I], BF16, name="w_bf")
+        nc.vector.scalar_tensor_tensor(
+            w_bf[:].rearrange("q (p t) -> q p t", t=PACK),
+            p_un[:].rearrange("q (p t) -> q p t", t=PACK),
+            inv_sum[:],
+            size_rows[:].rearrange("q t p -> q p t"),
+            ALU.mult, ALU.mult,
+        )
+
+        def turn(rows_bf, name):
+            words = rows_bf[:].bitcast(F32)
+            turned = psum2.tile([P, 2, P], F32, name="turned")
+            for u in range(2):
+                nc.tensor.transpose(turned[:, u, :], words[:, u : I // 2 : 2], ident[:])
+            grouped = held.tile([P, P, PACK], BF16, name=name + "_grouped", align_bytes=64)
+            nc.scalar.copy(grouped[:].rearrange("p c t -> p (c t)").bitcast(F32).rearrange("p (c u) -> p c u", u=2),
+                           turned[:].rearrange("p u c -> p c u"))
+            codes = held.tile([P, P], U32, name=name + "_codes", align_bytes=64)
+            scales = held.tile([P, P], U8, name=name + "_scales", align_bytes=64)
+            nc.vector.quantize_mx(codes[:].bitcast(FP8X4), scales[:], grouped[:].rearrange("p c t -> p (c t)"))
+            return codes, scales
+
+        w_codes, w_scales = turn(w_bf, "w")
+
+        for j in range(E // P):
+            val_bf = held.tile([P, I], BF16, name="val_bf%d" % j)
+            nc.vector.tensor_copy(val_bf[:], val_pool[j][:].indirect(offsets[:]))
+            v_codes, v_scales = turn(val_bf, "v%d" % j)
+            o_ps = psum2.tile([P, P], F32, name="o_ps")
+            nc.tensor.matmul_mx(o_ps[:], w_codes[:].bitcast(FP8X4), w_scales[:],
+                                v_codes[:].bitcast(FP8X4), v_scales[:], start=True, stop=True)
+            o_sb = held.tile([P, P], F32, name="o_sb%d" % j)
+            nc.scalar.copy(o_sb[:], o_ps[:])
+            nc.sync.dma_start(out[:, j * P : (j + 1) * P], o_sb[:])

@@ -21,17 +21,22 @@ P = 128
 PACK = 4
 
 
+HALF = I // 2
+
+
 def tile_attend_bestofviews_kernel(tc, query, query2, keys_words, keys_scales, keys2, size, vals, offs, out):
     nc = tc.nc
     with ExitStack() as ctx:
         held = ctx.enter_context(tc.tile_pool(name="held", bufs=1))
+        big = ctx.enter_context(tc.tile_pool(name="big", bufs=1))
         psum = ctx.enter_context(tc.psum_pool(name="psum", bufs=1))
         psum2 = ctx.enter_context(tc.psum_pool(name="psum2", bufs=2))
 
+        def slot_tile(slot, shape, dtype, name):
+            return big.tile(shape, dtype, name=name, tag="slot%d" % slot, align_bytes=64)
+
         offsets = held.tile([P, I // 16], U16, name="offsets")
-        key2_pool = [held.tile([P, T], F32, name="key2_pool%d" % t) for t in range(PACK)]
-        val_pool = [held.tile([P, T], F32, name="val_pool%d" % j) for j in range(E // P)]
-        word_pool = held.tile([P, T], I32, name="word_pool")
+        key2_pool = [slot_tile(t, [P, T], F32, "key2_pool%d" % t) for t in range(PACK)]
         scale_pool = held.tile([P, T], U8, name="scale_pool")
         q_raw = [held.tile([P, PACK, Q], F32, name="q_raw%d" % v) for v in range(2)]
         size_col = held.tile([P, PACK], F32, name="size_col")
@@ -39,22 +44,18 @@ def tile_attend_bestofviews_kernel(tc, query, query2, keys_words, keys_scales, k
         keys2_planes = keys2.rearrange("(p t) n -> t p n", t=PACK)
         nc.sync.dma_start(key2_pool[0][:], keys2_planes[0])
         nc.sync.dma_start(offsets[:], offs)
-        for t in range(1, 3):
-            nc.sync.dma_start(key2_pool[t][:], keys2_planes[t])
-        nc.vector.memset(scale_pool[:].bitcast(I32), 0)
+        nc.sync.dma_start(key2_pool[1][:], keys2_planes[1])
+        nc.gpsimd.memset(scale_pool[:].bitcast(I32), 0)
         for g in range(4):
             nc.sync.dma_start(
                 scale_pool[32 * g : 32 * g + 4, :].bitcast(I32),
                 keys_scales[0, 4 * g : 4 * g + 4, :].bitcast(I32),
             )
         nc.sync.dma_start(size_col[:], size.rearrange("o (p t) -> (o p) t", t=PACK))
-        nc.sync.dma_start(key2_pool[3][:], keys2_planes[3])
+        for t in range(2, 4):
+            nc.sync.dma_start(key2_pool[t][:], keys2_planes[t])
         nc.sync.dma_start(q_raw[1][:], query2.rearrange("(p t) q -> p t q", t=PACK))
         nc.sync.dma_start(q_raw[0][:], query.rearrange("(p t) q -> p t q", t=PACK))
-        nc.sync.dma_start(word_pool[:], keys_words[0].rearrange("p n t -> p (n t)").bitcast(I32))
-        for j in range(E // P):
-            nc.sync.dma_start(val_pool[j][:], vals[j * P : (j + 1) * P, :])
-
 
         warm = held.tile([P, 2], F32, name="warm")
         nc.vector.memset(warm[:, 0:1], 0.0)
@@ -68,15 +69,20 @@ def tile_attend_bestofviews_kernel(tc, query, query2, keys_words, keys_scales, k
             nc.tensor.transpose(size_rows[:, t, :], size_col[:, t : t + 1].to_broadcast([P, P]), ident[:])
 
         key_scales = held.tile([P, I], U8, name="key_scales", align_bytes=64)
-
         key2_bf = held.tile([P, I, PACK], BF16, name="key2_bf", align_bytes=64)
-        for t in range(PACK):
+        key2_pair = held.tile([P, 2, I], BF16, name="key2_pair")
+        for t in range(2):
+            nc.vector.tensor_copy(key2_pair[:, t, :], key2_pool[t][:].indirect(offsets[:]))
+        nc.scalar.copy(key2_bf[:, :, 0:2], key2_pair[:].rearrange("p t i -> p i t"))
+        nc.vector.tensor_copy(key_scales[:], scale_pool[:].indirect(offsets[:]))
+        for t in range(2, PACK):
             nc.vector.tensor_copy(key2_bf[:, :, t], key2_pool[t][:].indirect(offsets[:]))
-            if t == 2:
-                nc.vector.tensor_copy(key_scales[:], scale_pool[:].indirect(offsets[:]))
-        key2_codes = held.tile([P, I], U32, name="key2_codes", align_bytes=64)
-        key2_scales = held.tile([P, I], U8, name="key2_scales", align_bytes=64)
-        nc.vector.quantize_mx(key2_codes[:].bitcast(FP8X4), key2_scales[:], key2_bf[:].rearrange("p i t -> p (i t)"))
+
+        word_pool = slot_tile(0, [P, T], I32, "word_pool")
+        nc.sync.dma_start(word_pool[:], keys_words[0].rearrange("p n t -> p (n t)").bitcast(I32))
+        val_pool = [slot_tile(j + 1, [P, T], F32, "val_pool%d" % j) for j in range(3)]
+        for j in range(3):
+            nc.sync.dma_start(val_pool[j][:], vals[j * P : (j + 1) * P, :])
 
         q_bf = held.tile([P, 2, Q, PACK], BF16, name="q_bf", align_bytes=64)
         for v in (1, 0):
@@ -85,6 +91,10 @@ def tile_attend_bestofviews_kernel(tc, query, query2, keys_words, keys_scales, k
         q_scales = held.tile([P, 2 * Q], U8, name="q_scales", align_bytes=64)
         nc.vector.quantize_mx(q_codes[:].bitcast(FP8X4), q_scales[:], q_bf[:].rearrange("p v q t -> p (v q t)"))
 
+        key2_codes = held.tile([P, I], U32, name="key2_codes", align_bytes=64)
+        key2_scales = held.tile([P, I], U8, name="key2_scales", align_bytes=64)
+        nc.vector.quantize_mx(key2_codes[:].bitcast(FP8X4), key2_scales[:], key2_bf[:].rearrange("p i t -> p (i t)"))
+
         b_ps = psum.tile([P, I], F32, name="b_ps")
         nc.tensor.matmul_mx(b_ps[:], q_codes[:, Q:].bitcast(FP8X4), q_scales[:, Q:],
                             key2_codes[:].bitcast(FP8X4), key2_scales[:], start=True, stop=True)
@@ -92,25 +102,62 @@ def tile_attend_bestofviews_kernel(tc, query, query2, keys_words, keys_scales, k
         nc.scalar.copy(b_sb[:], b_ps[:])
 
         key_codes = held.tile([P, I], U32, name="key_codes", align_bytes=64)
-        nc.vector.tensor_copy(key_codes[:], word_pool[:].bitcast(U32).indirect(offsets[:]))
-        a_ps = psum.tile([P, I], F32, name="a_ps")
-        nc.tensor.matmul_mx(a_ps[:], q_codes[:, :Q].bitcast(FP8X4), q_scales[:, :Q],
-                            key_codes[:].bitcast(FP8X4), key_scales[:], start=True, stop=True)
+        a_ps = [psum.tile([P, HALF], F32, name="a_ps%d" % h) for h in range(2)]
+        halves = [slice(h * HALF, (h + 1) * HALF) for h in range(2)]
+        for h in range(2):
+            nc.vector.tensor_copy(key_codes[:, halves[h]],
+                                  word_pool[:].bitcast(U32).indirect(offsets[:, h * HALF // 16 : (h + 1) * HALF // 16]))
+            nc.tensor.matmul_mx(a_ps[h][:], q_codes[:, :Q].bitcast(FP8X4), q_scales[:, :Q],
+                                key_codes[:, halves[h]].bitcast(FP8X4), key_scales[:, halves[h]], start=True, stop=True)
+        val_pool.append(slot_tile(0, [P, T], F32, "val_pool3"))
+        nc.sync.dma_start(val_pool[3][:], vals[3 * P :, :])
 
         hi = held.tile([P, I], F32, name="hi")
         lo = held.tile([P, I], F32, name="lo")
-        s = held.tile([P, I], F32, name="s")
-        nc.vector.tensor_tensor(hi[:], a_ps[:], b_sb[:], ALU.max)
-        nc.vector.tensor_tensor(lo[:], a_ps[:], b_sb[:], ALU.min)
+        s = held.tile([P, I], F32, name="s", tag="s")
+        for h in range(2):
+            nc.vector.tensor_tensor(hi[:, halves[h]], a_ps[h][:], b_sb[:, halves[h]], ALU.max)
+            nc.vector.tensor_tensor(lo[:, halves[h]], a_ps[h][:], b_sb[:, halves[h]], ALU.min)
         nc.vector.scalar_tensor_tensor(s[:], lo[:], 0.5, hi[:], ALU.mult, ALU.add)
         neg_max = held.tile([P, 1], F32, name="neg_max")
         nc.vector.tensor_reduce(neg_max[:], s[:], AX.X, ALU.max, negate=True)
-        p_un = held.tile([P, I], F32, name="p_un")
+        val0_pool_bf = held.tile([P, T], BF16, name="val0_pool_bf")
+        nc.scalar.activation(val0_pool_bf[:], val_pool[0][:], ACT.Copy)
+        p_un = slot_tile(1, [P, I], F32, "p_un")
         row_sum = held.tile([P, 1], F32, name="row_sum")
         nc.scalar.activation(p_un[:], s[:], ACT.Exp, bias=neg_max[:], scale=1.0, accum_out=row_sum[:])
+
+        def gather_vals(j):
+            val_bf = held.tile([P, I], BF16, name="val_bf%d" % j)
+            nc.vector.tensor_copy(val_bf[:], val_pool[j][:].indirect(offsets[:]))
+            return val_bf
+
+        def turn(rows_bf, grouped):
+            words = rows_bf.bitcast(F32)
+            turned = psum2.tile([P, 2, P], F32, name="turned")
+            for u in range(2):
+                nc.tensor.transpose(turned[:, u, :], words[:, u : I // 2 : 2], ident[:])
+            nc.scalar.copy(grouped.bitcast(F32).rearrange("p (c u) -> p c u", u=2), turned[:].rearrange("p u c -> p c u"))
+
+        def product(cols, codes, scales):
+            width = cols.stop - cols.start
+            o_ps = psum2.tile([P, width], F32, name="o_ps")
+            nc.tensor.matmul_mx(o_ps[:], first_codes[:, :Q].bitcast(FP8X4), first_scales[:, :Q],
+                                codes.bitcast(FP8X4), scales, start=True, stop=True)
+            o_sb = held.tile([P, width], F32, name="o_sb%d" % cols.start)
+            nc.scalar.copy(o_sb[:], o_ps[:])
+            nc.sync.dma_start(out[:, cols], o_sb[:])
+
+        first_grouped = held.tile([P, 3 * I], BF16, name="first_grouped", align_bytes=64)
+        grouped = [held.tile([P, I], BF16, name="grouped%d" % j, align_bytes=64) for j in range(2)]
+
+        val0_bf = held.tile([P, I], BF16, name="val0_bf", tag="s")
+        nc.scalar.activation(val0_bf[:], val0_pool_bf[:].indirect(offsets[:]), ACT.Copy)
+        turn(gather_vals(1)[:], first_grouped[:, 2 * I :])
+
         inv_sum = held.tile([P, 1], F32, name="inv_sum")
         nc.vector.reciprocal(inv_sum[:], row_sum[:])
-        w_bf = held.tile([P, I], BF16, name="w_bf")
+        w_bf = slot_tile(2, [P, I], BF16, "w_bf")
         nc.vector.scalar_tensor_tensor(
             w_bf[:].rearrange("q (p t) -> q p t", t=PACK),
             p_un[:].rearrange("q (p t) -> q p t", t=PACK),
@@ -118,29 +165,18 @@ def tile_attend_bestofviews_kernel(tc, query, query2, keys_words, keys_scales, k
             size_rows[:].rearrange("q t p -> q p t"),
             ALU.mult, ALU.mult,
         )
-
-        def turn(rows_bf, name):
-            words = rows_bf[:].bitcast(F32)
-            turned = psum2.tile([P, 2, P], F32, name="turned")
-            for u in range(2):
-                nc.tensor.transpose(turned[:, u, :], words[:, u : I // 2 : 2], ident[:])
-            grouped = held.tile([P, P, PACK], BF16, name=name + "_grouped", align_bytes=64)
-            nc.scalar.copy(grouped[:].rearrange("p c t -> p (c t)").bitcast(F32).rearrange("p (c u) -> p c u", u=2),
-                           turned[:].rearrange("p u c -> p c u"))
-            codes = held.tile([P, P], U32, name=name + "_codes", align_bytes=64)
-            scales = held.tile([P, P], U8, name=name + "_scales", align_bytes=64)
-            nc.vector.quantize_mx(codes[:].bitcast(FP8X4), scales[:], grouped[:].rearrange("p c t -> p (c t)"))
-            return codes, scales
-
-        w_codes, w_scales = turn(w_bf, "w")
-
-        for j in range(E // P):
-            val_bf = held.tile([P, I], BF16, name="val_bf%d" % j)
-            nc.vector.tensor_copy(val_bf[:], val_pool[j][:].indirect(offsets[:]))
-            v_codes, v_scales = turn(val_bf, "v%d" % j)
-            o_ps = psum2.tile([P, P], F32, name="o_ps")
-            nc.tensor.matmul_mx(o_ps[:], w_codes[:].bitcast(FP8X4), w_scales[:],
-                                v_codes[:].bitcast(FP8X4), v_scales[:], start=True, stop=True)
-            o_sb = held.tile([P, P], F32, name="o_sb%d" % j)
-            nc.scalar.copy(o_sb[:], o_ps[:])
-            nc.sync.dma_start(out[:, j * P : (j + 1) * P], o_sb[:])
+        turn(val0_bf[:], first_grouped[:, I : 2 * I])
+        turn(w_bf[:], first_grouped[:, :I])
+        turn(gather_vals(2)[:], grouped[0][:])
+        first_codes = slot_tile(3, [P, 3 * P], U32, "first_codes")
+        first_scales = held.tile([P, 3 * P], U8, name="first_scales", align_bytes=64)
+        nc.vector.quantize_mx(first_codes[:, 2 * P :].bitcast(FP8X4), first_scales[:, 2 * P :], first_grouped[:, 2 * I :])
+        nc.vector.quantize_mx(first_codes[:, : 2 * P].bitcast(FP8X4), first_scales[:, : 2 * P], first_grouped[:, : 2 * I])
+        product(slice(0, 2 * P), first_codes[:, P:], first_scales[:, P:])
+        turn(gather_vals(3)[:], grouped[1][:])
+        codes2 = slot_tile(0, [P, P], U32, "codes2")
+        codes3 = held.tile([P, P], U32, name="codes3", align_bytes=64)
+        for j, codes in ((2, codes2), (3, codes3)):
+            scales = held.tile([P, P], U8, name="scales%d" % j, align_bytes=64)
+            nc.vector.quantize_mx(codes[:].bitcast(FP8X4), scales[:], grouped[j - 2][:])
+            product(slice(j * P, (j + 1) * P), codes[:], scales[:])

from contextlib import ExitStack

import concourse.mybir as mybir
from concourse.masks import make_identity

D, T, I, Q, E, K = 512, 2048, 512, 128, 512, 512
FLOPS = 2 * Q * I * (D + K + E)

F32 = mybir.dt.float32
BF16 = mybir.dt.bfloat16
I32 = mybir.dt.int32
U32 = mybir.dt.uint32
U16 = mybir.dt.uint16
U8 = mybir.dt.uint8
FP8X4 = mybir.dt.float8_e4m3fn_x4
ALU = mybir.AluOpType
ACT = mybir.ActivationFunctionType
AX = mybir.AxisListType

P = 128
PACK = 4


HALF = I // 2


def tile_attend_bestofviews_kernel(tc, query, query2, keys_words, keys_scales, keys2, size, vals, offs, out):
    nc = tc.nc
    with ExitStack() as ctx:
        held = ctx.enter_context(tc.tile_pool(name="held", bufs=1))
        big = ctx.enter_context(tc.tile_pool(name="big", bufs=1))
        psum = ctx.enter_context(tc.psum_pool(name="psum", bufs=1))
        psum2 = ctx.enter_context(tc.psum_pool(name="psum2", bufs=2))

        def slot_tile(slot, shape, dtype, name):
            return big.tile(shape, dtype, name=name, tag="slot%d" % slot, align_bytes=64)

        offsets = held.tile([P, I // 16], U16, name="offsets")
        key2_pool = [slot_tile(t, [P, T], F32, "key2_pool%d" % t) for t in range(PACK)]
        scale_pool = held.tile([P, T], U8, name="scale_pool")
        q_raw = [held.tile([P, PACK, Q], F32, name="q_raw%d" % v) for v in range(2)]
        size_col = held.tile([P, PACK], F32, name="size_col")

        keys2_planes = keys2.rearrange("(p t) n -> t p n", t=PACK)
        nc.sync.dma_start(key2_pool[0][:], keys2_planes[0])
        nc.sync.dma_start(offsets[:], offs)
        nc.sync.dma_start(key2_pool[1][:], keys2_planes[1])
        nc.gpsimd.memset(scale_pool[:].bitcast(I32), 0)
        for g in range(4):
            nc.sync.dma_start(
                scale_pool[32 * g : 32 * g + 4, :].bitcast(I32),
                keys_scales[0, 4 * g : 4 * g + 4, :].bitcast(I32),
            )
        nc.sync.dma_start(size_col[:], size.rearrange("o (p t) -> (o p) t", t=PACK))
        for t in range(2, 4):
            nc.sync.dma_start(key2_pool[t][:], keys2_planes[t])
        nc.sync.dma_start(q_raw[1][:], query2.rearrange("(p t) q -> p t q", t=PACK))
        nc.sync.dma_start(q_raw[0][:], query.rearrange("(p t) q -> p t q", t=PACK))

        warm = held.tile([P, 2], F32, name="warm")
        nc.vector.memset(warm[:, 0:1], 0.0)
        nc.scalar.activation(warm[:, 1:2], warm[:, 0:1], ACT.Exp)

        ident = held.tile([P, P], F32, name="ident")
        make_identity(nc, ident[:])

        size_rows = psum.tile([P, PACK, P], F32, name="size_rows")
        for t in range(PACK):
            nc.tensor.transpose(size_rows[:, t, :], size_col[:, t : t + 1].to_broadcast([P, P]), ident[:])

        key_scales = held.tile([P, I], U8, name="key_scales", align_bytes=64)
        key2_bf = held.tile([P, I, PACK], BF16, name="key2_bf", align_bytes=64)
        key2_pair = held.tile([P, 2, I], BF16, name="key2_pair")
        for t in range(2):
            nc.vector.tensor_copy(key2_pair[:, t, :], key2_pool[t][:].indirect(offsets[:]))
        nc.scalar.copy(key2_bf[:, :, 0:2], key2_pair[:].rearrange("p t i -> p i t"))
        nc.vector.tensor_copy(key_scales[:], scale_pool[:].indirect(offsets[:]))
        for t in range(2, PACK):
            nc.vector.tensor_copy(key2_bf[:, :, t], key2_pool[t][:].indirect(offsets[:]))

        word_pool = slot_tile(0, [P, T], I32, "word_pool")
        nc.sync.dma_start(word_pool[:], keys_words[0].rearrange("p n t -> p (n t)").bitcast(I32))
        val_pool = [slot_tile(j + 1, [P, T], F32, "val_pool%d" % j) for j in range(3)]
        for j in range(3):
            nc.sync.dma_start(val_pool[j][:], vals[j * P : (j + 1) * P, :])

        q_bf = held.tile([P, 2, Q, PACK], BF16, name="q_bf", align_bytes=64)
        for v in (1, 0):
            nc.scalar.copy(q_bf[:, v], q_raw[v][:].rearrange("p t q -> p q t"))
        q_codes = held.tile([P, 2 * Q], U32, name="q_codes", align_bytes=64)
        q_scales = held.tile([P, 2 * Q], U8, name="q_scales", align_bytes=64)
        nc.vector.quantize_mx(q_codes[:].bitcast(FP8X4), q_scales[:], q_bf[:].rearrange("p v q t -> p (v q t)"))

        key2_codes = held.tile([P, I], U32, name="key2_codes", align_bytes=64)
        key2_scales = held.tile([P, I], U8, name="key2_scales", align_bytes=64)
        nc.vector.quantize_mx(key2_codes[:].bitcast(FP8X4), key2_scales[:], key2_bf[:].rearrange("p i t -> p (i t)"))

        b_ps = psum.tile([P, I], F32, name="b_ps")
        nc.tensor.matmul_mx(b_ps[:], q_codes[:, Q:].bitcast(FP8X4), q_scales[:, Q:],
                            key2_codes[:].bitcast(FP8X4), key2_scales[:], start=True, stop=True)
        b_sb = held.tile([P, I], F32, name="b_sb")
        nc.scalar.copy(b_sb[:], b_ps[:])

        key_codes = held.tile([P, I], U32, name="key_codes", align_bytes=64)
        a_ps = [psum.tile([P, HALF], F32, name="a_ps%d" % h) for h in range(2)]
        halves = [slice(h * HALF, (h + 1) * HALF) for h in range(2)]
        for h in range(2):
            nc.vector.tensor_copy(key_codes[:, halves[h]],
                                  word_pool[:].bitcast(U32).indirect(offsets[:, h * HALF // 16 : (h + 1) * HALF // 16]))
            nc.tensor.matmul_mx(a_ps[h][:], q_codes[:, :Q].bitcast(FP8X4), q_scales[:, :Q],
                                key_codes[:, halves[h]].bitcast(FP8X4), key_scales[:, halves[h]], start=True, stop=True)
        val_pool.append(slot_tile(0, [P, T], F32, "val_pool3"))
        nc.sync.dma_start(val_pool[3][:], vals[3 * P :, :])

        hi = held.tile([P, I], F32, name="hi")
        lo = held.tile([P, I], F32, name="lo")
        s = held.tile([P, I], F32, name="s", tag="s")
        for h in range(2):
            nc.vector.tensor_tensor(hi[:, halves[h]], a_ps[h][:], b_sb[:, halves[h]], ALU.max)
            nc.vector.tensor_tensor(lo[:, halves[h]], a_ps[h][:], b_sb[:, halves[h]], ALU.min)
        nc.vector.scalar_tensor_tensor(s[:], lo[:], 0.5, hi[:], ALU.mult, ALU.add)
        neg_max = held.tile([P, 1], F32, name="neg_max")
        nc.vector.tensor_reduce(neg_max[:], s[:], AX.X, ALU.max, negate=True)
        val0_pool_bf = held.tile([P, T], BF16, name="val0_pool_bf")
        nc.scalar.activation(val0_pool_bf[:], val_pool[0][:], ACT.Copy)
        p_un = slot_tile(1, [P, I], F32, "p_un")
        row_sum = held.tile([P, 1], F32, name="row_sum")
        nc.scalar.activation(p_un[:], s[:], ACT.Exp, bias=neg_max[:], scale=1.0, accum_out=row_sum[:])

        def gather_vals(j):
            val_bf = held.tile([P, I], BF16, name="val_bf%d" % j)
            nc.vector.tensor_copy(val_bf[:], val_pool[j][:].indirect(offsets[:]))
            return val_bf

        def turn(rows_bf, grouped):
            words = rows_bf.bitcast(F32)
            turned = psum2.tile([P, 2, P], F32, name="turned")
            for u in range(2):
                nc.tensor.transpose(turned[:, u, :], words[:, u : I // 2 : 2], ident[:])
            nc.scalar.copy(grouped.bitcast(F32).rearrange("p (c u) -> p c u", u=2), turned[:].rearrange("p u c -> p c u"))

        def product(cols, codes, scales):
            width = cols.stop - cols.start
            o_ps = psum2.tile([P, width], F32, name="o_ps")
            nc.tensor.matmul_mx(o_ps[:], first_codes[:, :Q].bitcast(FP8X4), first_scales[:, :Q],
                                codes.bitcast(FP8X4), scales, start=True, stop=True)
            o_sb = held.tile([P, width], F32, name="o_sb%d" % cols.start)
            nc.scalar.copy(o_sb[:], o_ps[:])
            nc.sync.dma_start(out[:, cols], o_sb[:])

        first_grouped = held.tile([P, 3 * I], BF16, name="first_grouped", align_bytes=64)
        grouped = [held.tile([P, I], BF16, name="grouped%d" % j, align_bytes=64) for j in range(2)]

        val0_bf = held.tile([P, I], BF16, name="val0_bf", tag="s")
        nc.scalar.activation(val0_bf[:], val0_pool_bf[:].indirect(offsets[:]), ACT.Copy)
        turn(gather_vals(1)[:], first_grouped[:, 2 * I :])

        inv_sum = held.tile([P, 1], F32, name="inv_sum")
        nc.vector.reciprocal(inv_sum[:], row_sum[:])
        w_bf = slot_tile(2, [P, I], BF16, "w_bf")
        nc.vector.scalar_tensor_tensor(
            w_bf[:].rearrange("q (p t) -> q p t", t=PACK),
            p_un[:].rearrange("q (p t) -> q p t", t=PACK),
            inv_sum[:],
            size_rows[:].rearrange("q t p -> q p t"),
            ALU.mult, ALU.mult,
        )
        turn(val0_bf[:], first_grouped[:, I : 2 * I])
        turn(w_bf[:], first_grouped[:, :I])
        turn(gather_vals(2)[:], grouped[0][:])
        first_codes = slot_tile(3, [P, 3 * P], U32, "first_codes")
        first_scales = held.tile([P, 3 * P], U8, name="first_scales", align_bytes=64)
        nc.vector.quantize_mx(first_codes[:, 2 * P :].bitcast(FP8X4), first_scales[:, 2 * P :], first_grouped[:, 2 * I :])
        nc.vector.quantize_mx(first_codes[:, : 2 * P].bitcast(FP8X4), first_scales[:, : 2 * P], first_grouped[:, : 2 * I])
        product(slice(0, 2 * P), first_codes[:, P:], first_scales[:, P:])
        turn(gather_vals(3)[:], grouped[1][:])
        codes2 = slot_tile(0, [P, P], U32, "codes2")
        codes3 = held.tile([P, P], U32, name="codes3", align_bytes=64)
        for j, codes in ((2, codes2), (3, codes3)):
            scales = held.tile([P, P], U8, name="scales%d" % j, align_bytes=64)
            nc.vector.quantize_mx(codes[:].bitcast(FP8X4), scales[:], grouped[j - 2][:])
            product(slice(j * P, (j + 1) * P), codes[:], scales[:])
